import numpy as np
import ml_dtypes


def mxq(x, axis, fmt="e4m3"):
    dtype, down = {"e4m3": (ml_dtypes.float8_e4m3fn, 7), "e5m2": (ml_dtypes.float8_e5m2, 14)}[fmt]
    v = np.moveaxis(np.asarray(x, np.float32).astype(ml_dtypes.bfloat16).astype(np.float64), axis, -1)
    blocks = v.reshape(v.shape[:-1] + (-1, 32))
    amax = np.abs(blocks).max(-1, keepdims=True)
    byte = np.maximum(np.where(amax > 0, np.frexp(amax)[1] - 1 + 127, 0) - down, 1)
    scale = np.exp2(byte - 127.0)
    codes = (blocks / scale).astype(np.float32).astype(dtype).astype(np.float64)
    return np.moveaxis((codes * scale).reshape(v.shape), -1, axis)


WIDE = False


def mx_kscale(k):
    if not WIDE:
        return np.ones(k)
    levels = np.array([10, -10, 5, -5, 0])
    if k % 512:
        return np.exp2(np.random.permutation(np.resize(levels, k // 32))).repeat(32)
    a = np.empty((k // 512, 16))
    for p in range(k // 512):
        a[p, :8] = np.random.permutation(np.resize(levels, 8))
        for g in range(8):
            far = levels[np.abs(levels - a[p, g]) >= 10]
            a[p, g + 8] = far[np.random.randint(len(far))]
    return np.exp2(a.ravel()).repeat(32)


def f64(x):
    return np.asarray(x).astype(np.float64)


def striped(idx):
    return np.tile(np.asarray(idx).reshape(-1, 16).T, (8, 1)).astype(np.uint16)


def unstriped(offs):
    return offs[:16].T.reshape(-1).astype(np.int64)


B, N, T, D, DV, NQ = 1, 512, 1024, 512, 0, 512
PAGE = 128


def setup_inputs():
    n = np.random.standard_normal
    pages = np.random.permutation(T // PAGE)[:B * N // PAGE]
    idx = (pages[:, None] * PAGE + np.arange(PAGE)[None, :]).reshape(-1)
    s = mx_kscale(D)[:, None]
    r = np.random.uniform(0.5, 2.0, T)
    return {
        "qT": (n((B, D, NQ)) * s * (1.00 / np.sqrt(D))).astype(np.float32),
        "kT": (n((D, T)) / s / r).astype(np.float32),
        "ts": np.tile(r, (128, 1)).astype(np.float32),
        "offs": striped(idx),
    }


def reference(qT, kT, ts, offs):
    idx = unstriped(offs)
    pick = lambda x: x[:, idx].reshape(x.shape[0], B, N).transpose(1, 0, 2)
    a = mxq(f64(qT), 1, "e4m3").transpose(0, 2, 1) @ mxq(pick(f64(kT)), 1, "e4m3")
    a = a * pick(f64(ts))[:, :1, :]
    out = np.zeros((B, NQ, T))
    for b in range(B):
        out[b][:, idx[b * N:(b + 1) * N]] = a[b]
    return out

@@ -1,0 +1,103 @@
+from contextlib import ExitStack
+
+import concourse.mybir as mybir
+
+D_FEAT, NQ, T, N = 512, 512, 1024, 512
+P = 128
+PACK = 4
+FLOPS = 2 * D_FEAT * NQ * N
+
+F32 = mybir.dt.float32
+BF16 = mybir.dt.bfloat16
+U32 = mybir.dt.uint32
+U16 = mybir.dt.uint16
+U8 = mybir.dt.uint8
+FP8X4 = mybir.dt.float8_e4m3fn_x4
+MULT = mybir.AluOpType.mult
+
+
+def tile_attend_sddmm_ts_kernel(tc, qT, kT, ts, offs, out):
+    nc = tc.nc
+    k_rows = kT.rearrange("(p t) w -> p t w", t=PACK)
+    q_rows = qT.rearrange("b (p t) q -> p (b t) q", t=PACK)
+    out_rows = out.rearrange("b (m p) w -> p (b m) w", p=P)
+    half = N // 2
+
+    with ExitStack() as ctx:
+        keep = ctx.enter_context(tc.tile_pool(name="keep", bufs=1))
+        psum = ctx.enter_context(tc.psum_pool(name="psum", bufs=1))
+
+        offsets = keep.tile([P, N // 16], U16, name="offsets")
+        nc.sync.dma_start(offsets[:], offs)
+
+        k_pool = []
+        for t in range(PACK):
+            plane = keep.tile([P, T], F32, name="k_plane%d" % t)
+            nc.sync.dma_start(plane[:], k_rows[:, t, :])
+            k_pool.append(plane)
+
+        q_cuts = [(0, 128), (128, 128), (256, 256)]
+        q_raw = []
+        ts_pool = keep.tile([P, T], F32, name="ts_pool")
+        for i, (c0, w) in enumerate(q_cuts):
+            raw = keep.tile([P, PACK, w], F32, name="q_raw%d" % i)
+            nc.sync.dma_start(raw[:], q_rows[:, :, c0 : c0 + w])
+            q_raw.append(raw)
+            if i == 0:
+                nc.sync.dma_start(ts_pool[:], ts)
+
+        windows = []
+        for m in range(NQ // P):
+            window = keep.tile([P, T], F32, name="window%d" % m)
+            nc.vector.memset(window[:], 0.0)
+            windows.append(window)
+
+        g01 = keep.tile([P, 2, N], F32, name="g01")
+        g23 = keep.tile([P, 2, N], F32, name="g23")
+        k_grouped = keep.tile([P, N, PACK], BF16, name="k_grouped", align_bytes=64)
+        k_codes = keep.tile([P, N], U32, name="k_codes", align_bytes=64)
+        k_scales = keep.tile([P, N], U8, name="k_scales", align_bytes=64)
+        nc.vector.tensor_copy(g01[:, 0, :], k_pool[0][:].indirect(offsets[:]))
+        nc.vector.tensor_copy(g01[:, 1, :], k_pool[1][:].indirect(offsets[:]))
+        nc.scalar.copy(k_grouped[:, :, 0:2], g01[:].rearrange("p t c -> p c t"))
+        nc.vector.tensor_copy(g23[:, 0, :], k_pool[2][:].indirect(offsets[:]))
+        for h in range(2):
+            cols = slice(h * half, (h + 1) * half)
+            nc.vector.tensor_copy(g23[:, 1, cols], k_pool[3][:].indirect(offsets[:, h * (half // 16) : (h + 1) * (half // 16)]))
+        for h in range(2):
+            cols = slice(h * half, (h + 1) * half)
+            nc.vector.tensor_copy(k_grouped[:, cols, 2:4], g23[:, :, cols].rearrange("p t c -> p c t"))
+        for h in range(2):
+            cols = slice(h * half, (h + 1) * half)
+            nc.vector.quantize_mx(
+                out=k_codes[:, cols].bitcast(FP8X4),
+                scales=k_scales[:, cols],
+                in_=k_grouped[:, cols, :].rearrange("p c t -> p (c t)"),
+            )
+
+        q_codes, q_scales = [], []
+        ts_listed = keep.tile([P, N], F32, name="ts_listed")
+        for i, (c0, w) in enumerate(q_cuts):
+            grouped = keep.tile([P, w, PACK], BF16, name="q_grouped%d" % i, align_bytes=64)
+            nc.scalar.copy(grouped[:], q_raw[i][:].rearrange("p t c -> p c t"))
+            codes = keep.tile([P, w], U32, name="q_codes%d" % i, align_bytes=64)
+            scales = keep.tile([P, w], U8, name="q_scales%d" % i, align_bytes=64)
+            nc.vector.quantize_mx(out=codes[:].bitcast(FP8X4), scales=scales[:], in_=grouped[:].rearrange("p c t -> p (c t)"))
+            if i == 0:
+                nc.vector.tensor_copy(ts_listed[:], ts_pool[:].indirect(offsets[:]))
+            for m in range(c0 // P, (c0 + w) // P):
+                s = slice(m * P - c0, (m + 1) * P - c0)
+                acc = psum.tile([P, N], F32, name="acc%d" % m)
+                nc.tensor.matmul_mx(
+                    out=acc[:],
+                    lhsT=codes[:, s].bitcast(FP8X4),
+                    lhsT_scale=scales[:, s],
+                    rhs=k_codes[:].bitcast(FP8X4),
+                    rhs_scale=k_scales[:],
+                    start=True,
+                    stop=True,
+                )
+                scores = keep.tile([P, N], F32, name="scores%d" % m)
+                nc.scalar.copy(scores[:], acc[:])
+                nc.vector.tensor_tensor(windows[m][:].indirect(offsets[:]), scores[:], ts_listed[:], MULT)
+                nc.sync.dma_start(out_rows[:, m, :], windows[m][:])

@@ -36,14 +36,13 @@ def tile_attend_sddmm_ts_kernel(tc, qT, kT, ts, offs, out):
             nc.sync.dma_start(plane[:], k_rows[:, t, :])
             k_pool.append(plane)
 
-        q_cuts = [(0, 128), (128, 128), (256, 256)]
         q_raw = []
         ts_pool = keep.tile([P, T], F32, name="ts_pool")
-        for i, (c0, w) in enumerate(q_cuts):
-            raw = keep.tile([P, PACK, w], F32, name="q_raw%d" % i)
+        for c0, w in ((0, P), (P, P), (2 * P, 2 * P)):
+            raw = keep.tile([P, PACK, w], F32, name="q_raw%d" % c0)
             nc.sync.dma_start(raw[:], q_rows[:, :, c0 : c0 + w])
-            q_raw.append(raw)
-            if i == 0:
+            q_raw.extend(raw[:, :, c : c + P] for c in range(0, w, P))
+            if c0 == 0:
                 nc.sync.dma_start(ts_pool[:], ts)
 
         windows = []
@@ -51,6 +50,42 @@ def tile_attend_sddmm_ts_kernel(tc, qT, kT, ts, offs, out):
             window = keep.tile([P, T], F32, name="window%d" % m)
             nc.vector.memset(window[:], 0.0)
             windows.append(window)
+
+        q_codes, q_scales, q_grouped = {}, {}, {}
+
+        def group_queries(m):
+            tag = "q_codes%d" % (m - 2) if m >= 2 else "q_grouped%d" % m
+            grouped = keep.tile([P, P, PACK], BF16, name="q_grouped%d" % m, tag=tag, align_bytes=64)
+            nc.scalar.copy(grouped[:], q_raw[m].rearrange("p t c -> p c t"))
+            q_grouped[m] = grouped
+
+        def quantize_queries(m):
+            codes = keep.tile([P, P], U32, name="q_codes%d" % m, tag="q_codes%d" % m, align_bytes=64)
+            scales = keep.tile([P, P], U8, name="q_scales%d" % m, align_bytes=64)
+            nc.vector.quantize_mx(out=codes[:].bitcast(FP8X4), scales=scales[:], in_=q_grouped[m][:].rearrange("p c t -> p (c t)"))
+            q_codes[m], q_scales[m] = codes, scales
+
+        acc, scores = {}, {}
+
+        def multiply(m):
+            acc[m] = psum.tile([P, N], F32, name="acc%d" % m)
+            nc.tensor.matmul_mx(
+                out=acc[m][:],
+                lhsT=q_codes[m][:].bitcast(FP8X4),
+                lhsT_scale=q_scales[m][:],
+                rhs=k_codes[:].bitcast(FP8X4),
+                rhs_scale=k_scales[:],
+                start=True,
+                stop=True,
+            )
+
+        def empty(m):
+            scores[m] = keep.tile([P, N], F32, name="scores%d" % m)
+            nc.scalar.copy(scores[m][:], acc[m][:])
+
+        def place(m):
+            nc.vector.tensor_tensor(windows[m][:].indirect(offsets[:]), scores[m][:], ts_listed[:], MULT)
+            nc.sync.dma_start(out_rows[:, m, :], windows[m][:])
 
         g01 = keep.tile([P, 2, N], F32, name="g01")
         g23 = keep.tile([P, 2, N], F32, name="g23")
@@ -64,9 +99,11 @@ def tile_attend_sddmm_ts_kernel(tc, qT, kT, ts, offs, out):
         for h in range(2):
             cols = slice(h * half, (h + 1) * half)
             nc.vector.tensor_copy(g23[:, 1, cols], k_pool[3][:].indirect(offsets[:, h * (half // 16) : (h + 1) * (half // 16)]))
+        group_queries(0)
         for h in range(2):
             cols = slice(h * half, (h + 1) * half)
             nc.vector.tensor_copy(k_grouped[:, cols, 2:4], g23[:, :, cols].rearrange("p t c -> p c t"))
+        quantize_queries(0)
         for h in range(2):
             cols = slice(h * half, (h + 1) * half)
             nc.vector.quantize_mx(
@@ -74,30 +111,23 @@ def tile_attend_sddmm_ts_kernel(tc, qT, kT, ts, offs, out):
                 scales=k_scales[:, cols],
                 in_=k_grouped[:, cols, :].rearrange("p c t -> p (c t)"),
             )
-
-        q_codes, q_scales = [], []
+        group_queries(1)
+        quantize_queries(1)
         ts_listed = keep.tile([P, N], F32, name="ts_listed")
-        for i, (c0, w) in enumerate(q_cuts):
-            grouped = keep.tile([P, w, PACK], BF16, name="q_grouped%d" % i, align_bytes=64)
-            nc.scalar.copy(grouped[:], q_raw[i][:].rearrange("p t c -> p c t"))
-            codes = keep.tile([P, w], U32, name="q_codes%d" % i, align_bytes=64)
-            scales = keep.tile([P, w], U8, name="q_scales%d" % i, align_bytes=64)
-            nc.vector.quantize_mx(out=codes[:].bitcast(FP8X4), scales=scales[:], in_=grouped[:].rearrange("p c t -> p (c t)"))
-            if i == 0:
-                nc.vector.tensor_copy(ts_listed[:], ts_pool[:].indirect(offsets[:]))
-            for m in range(c0 // P, (c0 + w) // P):
-                s = slice(m * P - c0, (m + 1) * P - c0)
-                acc = psum.tile([P, N], F32, name="acc%d" % m)
-                nc.tensor.matmul_mx(
-                    out=acc[:],
-                    lhsT=codes[:, s].bitcast(FP8X4),
-                    lhsT_scale=scales[:, s],
-                    rhs=k_codes[:].bitcast(FP8X4),
-                    rhs_scale=k_scales[:],
-                    start=True,
-                    stop=True,
-                )
-                scores = keep.tile([P, N], F32, name="scores%d" % m)
-                nc.scalar.copy(scores[:], acc[:])
-                nc.vector.tensor_tensor(windows[m][:].indirect(offsets[:]), scores[:], ts_listed[:], MULT)
-                nc.sync.dma_start(out_rows[:, m, :], windows[m][:])
+        nc.vector.tensor_copy(ts_listed[:], ts_pool[:].indirect(offsets[:]))
+        multiply(0)
+        empty(0)
+        multiply(1)
+        group_queries(2)
+        place(0)
+        quantize_queries(2)
+        empty(1)
+        group_queries(3)
+        place(1)
+        quantize_queries(3)
+        multiply(2)
+        empty(2)
+        multiply(3)
+        empty(3)
+        place(2)
+        place(3)

@@ -38,17 +38,17 @@ def tile_attend_sddmm_ts_kernel(tc, qT, kT, ts, offs, out):
 
         q_raw = []
         ts_pool = keep.tile([P, T], F32, name="ts_pool")
-        for c0, w in ((0, P), (P, P), (2 * P, 2 * P)):
-            raw = keep.tile([P, PACK, w], F32, name="q_raw%d" % c0)
-            nc.sync.dma_start(raw[:], q_rows[:, :, c0 : c0 + w])
-            q_raw.extend(raw[:, :, c : c + P] for c in range(0, w, P))
+        for c0 in (0, 2 * P):
+            raw = keep.tile([P, PACK, 2 * P], F32, name="q_raw%d" % c0)
+            nc.sync.dma_start(raw[:], q_rows[:, :, c0 : c0 + 2 * P])
+            q_raw.extend(raw[:, :, c : c + P] for c in (0, P))
             if c0 == 0:
                 nc.sync.dma_start(ts_pool[:], ts)
 
         windows = []
         for m in range(NQ // P):
             window = keep.tile([P, T], F32, name="window%d" % m)
-            nc.vector.memset(window[:], 0.0)
+            nc.gpsimd.memset(window[:], 0.0)
             windows.append(window)
 
         q_codes, q_scales, q_grouped = {}, {}, {}
@@ -65,23 +65,26 @@ def tile_attend_sddmm_ts_kernel(tc, qT, kT, ts, offs, out):
             nc.vector.quantize_mx(out=codes[:].bitcast(FP8X4), scales=scales[:], in_=q_grouped[m][:].rearrange("p c t -> p (c t)"))
             q_codes[m], q_scales[m] = codes, scales
 
-        acc, scores = {}, {}
+        scores = {}
 
-        def multiply(m):
-            acc[m] = psum.tile([P, N], F32, name="acc%d" % m)
-            nc.tensor.matmul_mx(
-                out=acc[m][:],
-                lhsT=q_codes[m][:].bitcast(FP8X4),
-                lhsT_scale=q_scales[m][:],
-                rhs=k_codes[:].bitcast(FP8X4),
-                rhs_scale=k_scales[:],
-                start=True,
-                stop=True,
-            )
-
-        def empty(m):
+        def score(m, pieces):
             scores[m] = keep.tile([P, N], F32, name="scores%d" % m)
-            nc.scalar.copy(scores[m][:], acc[m][:])
+            width = N // pieces
+            for h in range(pieces):
+                cols = slice(h * width, (h + 1) * width)
+                if pieces == 2:
+                    quantize_keys(cols)
+                acc = psum.tile([P, width], F32, name="acc%d_%d" % (m, h))
+                nc.tensor.matmul_mx(
+                    out=acc[:],
+                    lhsT=q_codes[m][:].bitcast(FP8X4),
+                    lhsT_scale=q_scales[m][:],
+                    rhs=k_codes[:, cols].bitcast(FP8X4),
+                    rhs_scale=k_scales[:, cols],
+                    start=True,
+                    stop=True,
+                )
+                nc.scalar.copy(scores[m][:, cols], acc[:])
 
         def place(m):
             nc.vector.tensor_tensor(windows[m][:].indirect(offsets[:]), scores[m][:], ts_listed[:], MULT)
@@ -92,6 +95,14 @@ def tile_attend_sddmm_ts_kernel(tc, qT, kT, ts, offs, out):
         k_grouped = keep.tile([P, N, PACK], BF16, name="k_grouped", align_bytes=64)
         k_codes = keep.tile([P, N], U32, name="k_codes", align_bytes=64)
         k_scales = keep.tile([P, N], U8, name="k_scales", align_bytes=64)
+
+        def quantize_keys(cols):
+            nc.vector.quantize_mx(
+                out=k_codes[:, cols].bitcast(FP8X4),
+                scales=k_scales[:, cols],
+                in_=k_grouped[:, cols, :].rearrange("p c t -> p (c t)"),
+            )
+
         nc.vector.tensor_copy(g01[:, 0, :], k_pool[0][:].indirect(offsets[:]))
         nc.vector.tensor_copy(g01[:, 1, :], k_pool[1][:].indirect(offsets[:]))
         nc.scalar.copy(k_grouped[:, :, 0:2], g01[:].rearrange("p t c -> p c t"))
@@ -99,35 +110,23 @@ def tile_attend_sddmm_ts_kernel(tc, qT, kT, ts, offs, out):
         for h in range(2):
             cols = slice(h * half, (h + 1) * half)
             nc.vector.tensor_copy(g23[:, 1, cols], k_pool[3][:].indirect(offsets[:, h * (half // 16) : (h + 1) * (half // 16)]))
+        for copy, cols in ((nc.scalar.copy, slice(384, 512)), (nc.vector.tensor_copy, slice(0, 256)), (nc.vector.tensor_copy, slice(256, 384))):
+            copy(k_grouped[:, cols, 2:4], g23[:, :, cols].rearrange("p t c -> p c t"))
         group_queries(0)
-        for h in range(2):
-            cols = slice(h * half, (h + 1) * half)
-            nc.vector.tensor_copy(k_grouped[:, cols, 2:4], g23[:, :, cols].rearrange("p t c -> p c t"))
         quantize_queries(0)
-        for h in range(2):
-            cols = slice(h * half, (h + 1) * half)
-            nc.vector.quantize_mx(
-                out=k_codes[:, cols].bitcast(FP8X4),
-                scales=k_scales[:, cols],
-                in_=k_grouped[:, cols, :].rearrange("p c t -> p (c t)"),
-            )
         group_queries(1)
+        score(0, 2)
         quantize_queries(1)
         ts_listed = keep.tile([P, N], F32, name="ts_listed")
         nc.vector.tensor_copy(ts_listed[:], ts_pool[:].indirect(offsets[:]))
-        multiply(0)
-        empty(0)
-        multiply(1)
         group_queries(2)
         place(0)
         quantize_queries(2)
-        empty(1)
+        score(1, 1)
         group_queries(3)
         place(1)
         quantize_queries(3)
-        multiply(2)
-        empty(2)
-        multiply(3)
-        empty(3)
+        score(2, 1)
+        score(3, 1)
         place(2)
         place(3)

@@ -38,10 +38,10 @@ def tile_attend_sddmm_ts_kernel(tc, qT, kT, ts, offs, out):
 
         q_raw = []
         ts_pool = keep.tile([P, T], F32, name="ts_pool")
-        for c0 in (0, 2 * P):
-            raw = keep.tile([P, PACK, 2 * P], F32, name="q_raw%d" % c0)
-            nc.sync.dma_start(raw[:], q_rows[:, :, c0 : c0 + 2 * P])
-            q_raw.extend(raw[:, :, c : c + P] for c in (0, P))
+        for c0, w in ((0, 2 * P), (2 * P, P), (3 * P, P)):
+            raw = keep.tile([P, PACK, w], F32, name="q_raw%d" % c0)
+            nc.sync.dma_start(raw[:], q_rows[:, :, c0 : c0 + w])
+            q_raw.extend(raw[:, :, c : c + P] for c in range(0, w, P))
             if c0 == 0:
                 nc.sync.dma_start(ts_pool[:], ts)
 
@@ -54,13 +54,12 @@ def tile_attend_sddmm_ts_kernel(tc, qT, kT, ts, offs, out):
         q_codes, q_scales, q_grouped = {}, {}, {}
 
         def group_queries(m):
-            tag = "q_codes%d" % (m - 2) if m >= 2 else "q_grouped%d" % m
-            grouped = keep.tile([P, P, PACK], BF16, name="q_grouped%d" % m, tag=tag, align_bytes=64)
+            grouped = keep.tile([P, P, PACK], BF16, name="q_grouped%d" % m, align_bytes=64)
             nc.scalar.copy(grouped[:], q_raw[m].rearrange("p t c -> p c t"))
             q_grouped[m] = grouped
 
         def quantize_queries(m):
-            codes = keep.tile([P, P], U32, name="q_codes%d" % m, tag="q_codes%d" % m, align_bytes=64)
+            codes = keep.tile([P, P], U32, name="q_codes%d" % m, align_bytes=64)
             scales = keep.tile([P, P], U8, name="q_scales%d" % m, align_bytes=64)
             nc.vector.quantize_mx(out=codes[:].bitcast(FP8X4), scales=scales[:], in_=q_grouped[m][:].rearrange("p c t -> p (c t)"))
             q_codes[m], q_scales[m] = codes, scales
@@ -68,7 +67,8 @@ def tile_attend_sddmm_ts_kernel(tc, qT, kT, ts, offs, out):
         scores = {}
 
         def score(m, pieces):
-            scores[m] = keep.tile([P, N], F32, name="scores%d" % m)
+            tag = "q_raw%d" % ((m + 1) * P) if m in (1, 2) else "scores%d" % m
+            scores[m] = keep.tile([P, N], F32, name="scores%d" % m, tag=tag)
             width = N // pieces
             for h in range(pieces):
                 cols = slice(h * width, (h + 1) * width)
@@ -124,9 +124,9 @@ def tile_attend_sddmm_ts_kernel(tc, qT, kT, ts, offs, out):
         quantize_queries(2)
         score(1, 1)
         group_queries(3)
-        place(1)
         quantize_queries(3)
+        place(1)
         score(2, 1)
-        score(3, 1)
         place(2)
+        score(3, 1)
         place(3)

from contextlib import ExitStack

import concourse.mybir as mybir

D_FEAT, NQ, T, N = 512, 512, 1024, 512
P = 128
PACK = 4
FLOPS = 2 * D_FEAT * NQ * N

F32 = mybir.dt.float32
BF16 = mybir.dt.bfloat16
U32 = mybir.dt.uint32
U16 = mybir.dt.uint16
U8 = mybir.dt.uint8
FP8X4 = mybir.dt.float8_e4m3fn_x4
MULT = mybir.AluOpType.mult


def tile_attend_sddmm_ts_kernel(tc, qT, kT, ts, offs, out):
    nc = tc.nc
    k_rows = kT.rearrange("(p t) w -> p t w", t=PACK)
    q_rows = qT.rearrange("b (p t) q -> p (b t) q", t=PACK)
    out_rows = out.rearrange("b (m p) w -> p (b m) w", p=P)
    half = N // 2

    with ExitStack() as ctx:
        keep = ctx.enter_context(tc.tile_pool(name="keep", bufs=1))
        psum = ctx.enter_context(tc.psum_pool(name="psum", bufs=1))

        offsets = keep.tile([P, N // 16], U16, name="offsets")
        nc.sync.dma_start(offsets[:], offs)

        k_pool = []
        for t in range(PACK):
            plane = keep.tile([P, T], F32, name="k_plane%d" % t)
            nc.sync.dma_start(plane[:], k_rows[:, t, :])
            k_pool.append(plane)

        q_raw = []
        ts_pool = keep.tile([P, T], F32, name="ts_pool")
        for c0, w in ((0, 2 * P), (2 * P, P), (3 * P, P)):
            raw = keep.tile([P, PACK, w], F32, name="q_raw%d" % c0)
            nc.sync.dma_start(raw[:], q_rows[:, :, c0 : c0 + w])
            q_raw.extend(raw[:, :, c : c + P] for c in range(0, w, P))
            if c0 == 0:
                nc.sync.dma_start(ts_pool[:], ts)

        windows = []
        for m in range(NQ // P):
            window = keep.tile([P, T], F32, name="window%d" % m)
            nc.gpsimd.memset(window[:], 0.0)
            windows.append(window)

        q_codes, q_scales, q_grouped = {}, {}, {}

        def group_queries(m):
            grouped = keep.tile([P, P, PACK], BF16, name="q_grouped%d" % m, align_bytes=64)
            nc.scalar.copy(grouped[:], q_raw[m].rearrange("p t c -> p c t"))
            q_grouped[m] = grouped

        def quantize_queries(m):
            codes = keep.tile([P, P], U32, name="q_codes%d" % m, align_bytes=64)
            scales = keep.tile([P, P], U8, name="q_scales%d" % m, align_bytes=64)
            nc.vector.quantize_mx(out=codes[:].bitcast(FP8X4), scales=scales[:], in_=q_grouped[m][:].rearrange("p c t -> p (c t)"))
            q_codes[m], q_scales[m] = codes, scales

        scores = {}

        def score(m, pieces):
            tag = "q_raw%d" % ((m + 1) * P) if m in (1, 2) else "scores%d" % m
            scores[m] = keep.tile([P, N], F32, name="scores%d" % m, tag=tag)
            width = N // pieces
            for h in range(pieces):
                cols = slice(h * width, (h + 1) * width)
                if pieces == 2:
                    quantize_keys(cols)
                acc = psum.tile([P, width], F32, name="acc%d_%d" % (m, h))
                nc.tensor.matmul_mx(
                    out=acc[:],
                    lhsT=q_codes[m][:].bitcast(FP8X4),
                    lhsT_scale=q_scales[m][:],
                    rhs=k_codes[:, cols].bitcast(FP8X4),
                    rhs_scale=k_scales[:, cols],
                    start=True,
                    stop=True,
                )
                nc.scalar.copy(scores[m][:, cols], acc[:])

        def place(m):
            nc.vector.tensor_tensor(windows[m][:].indirect(offsets[:]), scores[m][:], ts_listed[:], MULT)
            nc.sync.dma_start(out_rows[:, m, :], windows[m][:])

        g01 = keep.tile([P, 2, N], F32, name="g01")
        g23 = keep.tile([P, 2, N], F32, name="g23")
        k_grouped = keep.tile([P, N, PACK], BF16, name="k_grouped", align_bytes=64)
        k_codes = keep.tile([P, N], U32, name="k_codes", align_bytes=64)
        k_scales = keep.tile([P, N], U8, name="k_scales", align_bytes=64)

        def quantize_keys(cols):
            nc.vector.quantize_mx(
                out=k_codes[:, cols].bitcast(FP8X4),
                scales=k_scales[:, cols],
                in_=k_grouped[:, cols, :].rearrange("p c t -> p (c t)"),
            )

        nc.vector.tensor_copy(g01[:, 0, :], k_pool[0][:].indirect(offsets[:]))
        nc.vector.tensor_copy(g01[:, 1, :], k_pool[1][:].indirect(offsets[:]))
        nc.scalar.copy(k_grouped[:, :, 0:2], g01[:].rearrange("p t c -> p c t"))
        nc.vector.tensor_copy(g23[:, 0, :], k_pool[2][:].indirect(offsets[:]))
        for h in range(2):
            cols = slice(h * half, (h + 1) * half)
            nc.vector.tensor_copy(g23[:, 1, cols], k_pool[3][:].indirect(offsets[:, h * (half // 16) : (h + 1) * (half // 16)]))
        for copy, cols in ((nc.scalar.copy, slice(384, 512)), (nc.vector.tensor_copy, slice(0, 256)), (nc.vector.tensor_copy, slice(256, 384))):
            copy(k_grouped[:, cols, 2:4], g23[:, :, cols].rearrange("p t c -> p c t"))
        group_queries(0)
        quantize_queries(0)
        group_queries(1)
        score(0, 2)
        quantize_queries(1)
        ts_listed = keep.tile([P, N], F32, name="ts_listed")
        nc.vector.tensor_copy(ts_listed[:], ts_pool[:].indirect(offsets[:]))
        group_queries(2)
        place(0)
        quantize_queries(2)
        score(1, 1)
        group_queries(3)
        quantize_queries(3)
        place(1)
        score(2, 1)
        place(2)
        score(3, 1)
        place(3)
